import numpy as np
import ml_dtypes


def mxq(x, axis, fmt="e4m3"):
    dtype, down = {"e4m3": (ml_dtypes.float8_e4m3fn, 7), "e5m2": (ml_dtypes.float8_e5m2, 14)}[fmt]
    v = np.moveaxis(np.asarray(x, np.float32).astype(ml_dtypes.bfloat16).astype(np.float64), axis, -1)
    blocks = v.reshape(v.shape[:-1] + (-1, 32))
    amax = np.abs(blocks).max(-1, keepdims=True)
    byte = np.maximum(np.where(amax > 0, np.frexp(amax)[1] - 1 + 127, 0) - down, 1)
    scale = np.exp2(byte - 127.0)
    codes = (blocks / scale).astype(np.float32).astype(dtype).astype(np.float64)
    return np.moveaxis((codes * scale).reshape(v.shape), -1, axis)


WIDE = False


def mx_kscale(k):
    if not WIDE:
        return np.ones(k)
    levels = np.array([30, -30])
    if k % 512:
        return np.exp2(np.random.permutation(np.resize(levels, k // 32))).repeat(32)
    a = np.empty((k // 512, 16))
    for p in range(k // 512):
        a[p, :8] = np.random.permutation(np.resize(levels, 8))
        for g in range(8):
            far = levels[np.abs(levels - a[p, g]) >= 10]
            a[p, g + 8] = far[np.random.randint(len(far))]
    return np.exp2(a.ravel()).repeat(32)


def f64(x):
    return np.asarray(x).astype(np.float64)


def striped(idx):
    return np.tile(np.asarray(idx).reshape(-1, 16).T, (8, 1)).astype(np.uint16)


def unstriped(offs):
    return offs[:16].T.reshape(-1).astype(np.int64)


E2M1 = np.array([0.0, 0.5, 1.0, 1.5, 2.0, 3.0, 4.0, 6.0, -0.0, -0.5, -1.0, -1.5, -2.0, -3.0, -4.0, -6.0])


def pack_weight(w, fmt):
    k, n = w.shape
    w = f64(np.asarray(w, np.float32).astype(ml_dtypes.bfloat16)).reshape(k // 32, 32, n)
    amax = np.abs(w).max(1)
    if fmt == "e4m3":
        byte = np.frexp(amax)[1] - 1 + 127 - 7
    else:
        mant, ex = np.frexp(amax / 6.0)
        byte = np.where(mant > 0.5, ex, ex - 1) + 127
    byte = np.clip(np.where(amax > 0, byte, 1), 1, 254)
    scaled = (w * np.exp2(127.0 - byte)[:, None, :]).reshape(k, n).astype(np.float32)
    by_word = np.ascontiguousarray(scaled.reshape(k // 512, 128, 4, n).transpose(0, 1, 3, 2))
    if fmt == "e4m3":
        words = by_word.astype(ml_dtypes.float8_e4m3fn).view(np.uint8)
    else:
        c = by_word.astype(ml_dtypes.float4_e2m1fn).view(np.uint8) & 0xF
        words = (c[..., 0::2] | (c[..., 1::2] << 4)).reshape(k // 512, 128, 2 * n)
    return np.ascontiguousarray(words), np.ascontiguousarray(byte.astype(np.uint8).reshape(k // 512, 16, n))


def unpack_weight(words, scales, fmt):
    g, _, n = scales.shape
    words = np.ascontiguousarray(words).reshape(g, 128, n, -1)
    if fmt == "e4m3":
        vals = words.view(ml_dtypes.float8_e4m3fn).astype(np.float64)
    else:
        nib = np.empty((g, 128, n, 4), np.uint8)
        nib[..., 0::2] = words & 0xF
        nib[..., 1::2] = words >> 4
        vals = E2M1[nib]
    vals = vals * np.repeat(np.exp2(scales.astype(np.float64) - 127.0), 8, axis=1)[..., None]
    return vals.transpose(0, 1, 3, 2).reshape(g * 512, n)


K, T, J, I, V, L = 1024, 1024, 256, 256, 1024, 512


def setup_inputs():
    n = np.random.standard_normal
    idx = np.random.permutation(T)[:J]
    idx2 = np.random.permutation(V)[:I]
    fk = mx_kscale(K)
    fl = mx_kscale(L)
    kyp = pack_weight(n((K, V)) / fk[:, None], "e2m1")
    cxp = pack_weight(n((L, J)) / fl[:, None], "e2m1")
    wcp = pack_weight(n((L, I)) * 1 / np.sqrt(L) * fl[:, None], "e4m3")
    return {
        "xf": (n((K, T)) * 0.03).astype(np.float32),
        "fk": (np.random.uniform(0.5, 2.0, (K, 1)) * fk[:, None]).astype(np.float32),
        "ky_words": kyp[0],
        "ky_scales": kyp[1],
        "bi": (np.random.uniform(-0.7, 0.7, (1, I))).astype(np.float32),
        "cx_words": cxp[0],
        "cx_scales": cxp[1],
        "wc_words": wcp[0],
        "wc_scales": wcp[1],
        "offs": striped(idx),
        "offs2": striped(idx2),
    }


def reference(xf, fk, ky_words, ky_scales, bi, cx_words, cx_scales, wc_words, wc_scales, offs, offs2):
    idx = unstriped(offs)
    idx2 = unstriped(offs2)
    kyu = unpack_weight(ky_words, ky_scales, "e2m1")
    cxu = unpack_weight(cx_words, cx_scales, "e2m1")
    wcu = unpack_weight(wc_words, wc_scales, "e4m3")
    xg = f64(xf)[:, idx]
    x1 = np.pad(xg, ((0, 0), (1, 0)))[:, :J]
    u = (xg - 0.6 * x1) * f64(fk)
    uq = mxq(u, 0, "e5m2")
    kyidx2g = kyu[:, idx2]
    a0 = uq.T @ kyidx2g
    a = a0 + f64(bi)
    q = cxu.T @ wcu
    y = np.maximum(a, q) - 0.5 * np.minimum(a, q)
    return y

@@ -1,0 +1,211 @@
+from contextlib import ExitStack
+
+import concourse.mybir as mybir
+
+K, T, J, I, V, L = 1024, 1024, 256, 256, 1024, 512
+FLOPS = 2 * K * J * I + 2 * L * J * I
+
+F32 = mybir.dt.float32
+BF16 = mybir.dt.bfloat16
+I32 = mybir.dt.int32
+U32 = mybir.dt.uint32
+U16 = mybir.dt.uint16
+U8 = mybir.dt.uint8
+E5M2 = mybir.dt.float8_e5m2_x4
+E4M3 = mybir.dt.float8_e4m3fn_x4
+E2M1 = mybir.dt.float4_e2m1fn_x4
+ALU = mybir.AluOpType
+COPY = mybir.ActivationFunctionType.Copy
+
+P = 128
+PACK = 4
+PASSES = K // (P * PACK)
+HALVES = J // P
+PAD = 8
+LIST_COLS = P // 16
+QUAD = 32
+BI_RUN = I // QUAD
+
+
+def tile_list_scores_steps_listed_tworank_kernel(
+    tc, xf, fk, ky_words, ky_scales, bi, cx_words, cx_scales, wc_words, wc_scales, offs, offs2, out
+):
+    nc = tc.nc
+    with ExitStack() as ctx:
+        sb = ctx.enter_context(tc.tile_pool(name="sb", bufs=1))
+        ps = ctx.enter_context(tc.psum_pool(name="ps", bufs=1))
+
+        tok = sb.tile([P, J // 16], U16, name="tok")
+        key = sb.tile([P, I // 16], U16, name="key")
+        fk_sb = sb.tile([P, PASSES, PACK], F32, name="fk_sb")
+        bi_runs = sb.tile([P, BI_RUN], F32, name="bi_runs")
+        x = [[sb.tile([P, T], F32, name="x%d%d" % (z, t)) for t in range(PACK)] for z in range(PASSES)]
+        ky_w = [sb.tile([P, V], U16, name="ky_w%d" % z, align_bytes=64) for z in range(PASSES)]
+        ky_s = sb.tile([P, PASSES, V], U8, name="ky_s", align_bytes=64)
+        cx_w = sb.tile([P, J], U16, name="cx_w", align_bytes=64)
+        wc_w = sb.tile([P, I], U32, name="wc_w", align_bytes=64)
+        cx_s = sb.tile([P, J], U8, name="cx_s", align_bytes=64)
+        wc_s = sb.tile([P, I], U8, name="wc_s", align_bytes=64)
+        picked = sb.tile([P, PASSES * PACK, PAD + J], F32, name="picked")
+
+        nc.vector.memset(cx_s[:].bitcast(I32), 0)
+        nc.vector.memset(ky_s[:].rearrange("p z c -> p (z c)").bitcast(I32), 0)
+        nc.vector.memset(wc_s[:].bitcast(I32), 0)
+        nc.vector.memset(picked[:, :, PAD - 1 : PAD], 0.0)
+
+        rows = xf.rearrange("(z p t) w -> z t p w", z=PASSES, t=PACK)
+
+        def load_x(n):
+            nc.sync.dma_start(x[n // PACK][n % PACK][:], rows[n // PACK, n % PACK])
+
+        def load_scales(queue, plane, src, quad):
+            queue.dma_start(
+                plane[QUAD * quad : QUAD * quad + 4, :].bitcast(I32), src[0, 4 * quad : 4 * quad + 4, :].bitcast(I32)
+            )
+
+        def load_ky_scales(quad):
+            nc.sync.dma_start(
+                ky_s[QUAD * quad : QUAD * quad + 4, :, :].bitcast(I32),
+                ky_scales[:, 4 * quad : 4 * quad + 4, :].rearrange("z r c -> r z c").bitcast(I32),
+            )
+
+        for quad in range(4):
+            load_scales(nc.gpsimd, cx_s, cx_scales, quad)
+
+        nc.sync.dma_start(tok[:], offs)
+        nc.sync.dma_start(key[:], offs2)
+        nc.sync.dma_start(
+            bi_runs[:], bi[0].rearrange("(c b) -> c b", b=BI_RUN).unsqueeze(0).to_broadcast([P // QUAD, QUAD, BI_RUN])
+        )
+        for z in range(PASSES):
+            nc.sync.dma_start(ky_w[z][:].bitcast(I32), ky_words[z].bitcast(I32))
+        load_x(0)
+        nc.sync.dma_start(fk_sb[:], fk.rearrange("(z p t) o -> p z (t o)", z=PASSES, t=PACK))
+        load_ky_scales(0)
+        load_ky_scales(1)
+        load_x(1)
+        load_ky_scales(2)
+        load_ky_scales(3)
+        load_scales(nc.sync, wc_s, wc_scales, 0)
+        load_x(2)
+        for quad in range(1, 4):
+            load_scales(nc.sync, wc_s, wc_scales, quad)
+        nc.sync.dma_start(cx_w[:].bitcast(I32), cx_words[0].bitcast(I32))
+        nc.sync.dma_start(wc_w[:].bitcast(I32), wc_words[0].rearrange("p n t -> p (n t)").bitcast(I32))
+        for n in range(3, 8):
+            load_x(n)
+
+        u_codes = sb.tile([P, PASSES, J], U32, name="u_codes", align_bytes=64)
+        u_scales = sb.tile([P, PASSES, J], U8, name="u_scales", align_bytes=64)
+        ky_wg = [sb.tile([P, I], U16, name="ky_wg%d" % z, align_bytes=64) for z in range(PASSES)]
+        ky_sg = sb.tile([P, PASSES, I], U8, name="ky_sg", align_bytes=64)
+
+        def product(z, h):
+            rows_j = slice(h * P, (h + 1) * P)
+            nc.tensor.matmul_mx(
+                out=a_bank[h][:],
+                lhsT=u_codes[:, z, rows_j].bitcast(E5M2),
+                lhsT_scale=u_scales[:, z, rows_j],
+                rhs=ky_wg[z][:].bitcast(E2M1),
+                rhs_scale=ky_sg[:, z, :],
+                start=(z == 0),
+                stop=(z == PASSES - 1),
+            )
+
+        for z in range(PASSES):
+            nc.vector.tensor_copy(ky_wg[z][:], ky_w[z][:].indirect(key[:]))
+        for z in range(PASSES):
+            nc.vector.tensor_copy(ky_sg[:, z, :], ky_s[:, z, :].indirect(key[:]))
+
+        raw = sb.tile([P, PACK, J], F32, name="raw")
+        u_flat = sb.tile([P, PACK, J], BF16, name="u_flat")
+        u0 = sb.tile([P, J, PACK], BF16, name="u0", align_bytes=64)
+        for t in range(PACK):
+            nc.scalar.activation(raw[:, t, :], x[0][t][:].indirect(tok[:]), COPY)
+            nc.scalar.activation(picked[:, t, PAD:], raw[:, t, :], COPY, scale=fk_sb[:, 0, t : t + 1])
+            nc.vector.scalar_tensor_tensor(
+                u_flat[:, t, :], picked[:, t, PAD - 1 : PAD - 1 + J], -0.6, picked[:, t, PAD:], ALU.mult, ALU.add
+            )
+            if t % 2 == 1:
+                nc.vector.tensor_copy(
+                    u0[:, :, t - 1 : t + 1].rearrange("p (c i) t -> p c t i", i=2),
+                    u_flat[:, t - 1 : t + 1, :].rearrange("p t (c i) -> p c t i", i=2),
+                )
+        nc.vector.quantize_mx(
+            out=u_codes[:, 0, :].bitcast(E5M2), scales=u_scales[:, 0, :], in_=u0[:].rearrange("p j t -> p (j t)")
+        )
+
+        step = sb.tile([P, PACK, J], F32, name="step")
+        u1 = [sb.tile([P, P, PACK], BF16, name="u1_%d" % h, align_bytes=64) for h in range(HALVES)]
+
+        def late_plane(t):
+            row = picked[:, PACK + t, :]
+            for h in range(HALVES):
+                window = x[1][t][:].indirect(tok[:, h * LIST_COLS : (h + 1) * LIST_COLS])
+                dst = row[:, PAD + h * P : PAD + (h + 1) * P]
+                if t == PACK - 1 and h == 0:
+                    nc.vector.tensor_copy(dst, window)
+                else:
+                    nc.scalar.activation(dst, window, COPY)
+            for h in range(HALVES):
+                lo = PAD + h * P
+                nc.vector.scalar_tensor_tensor(
+                    step[:, t, h * P : (h + 1) * P], row[:, lo - 1 : lo - 1 + P], -0.6, row[:, lo : lo + P], ALU.mult, ALU.add
+                )
+            for h in range(HALVES):
+                nc.vector.tensor_scalar(
+                    u1[h][:, :, t], step[:, t, h * P : (h + 1) * P], fk_sb[:, 1, t : t + 1], None, ALU.mult
+                )
+
+        late_plane(0)
+
+        bi_wide = sb.tile([P, BI_RUN, QUAD], F32, name="bi_wide", align_bytes=64)
+        bi_all = sb.tile([P, BI_RUN, QUAD], F32, name="bi_all", align_bytes=64)
+        nc.vector.tensor_copy(bi_wide[:], bi_runs[:].unsqueeze(2).to_broadcast([P, BI_RUN, QUAD]))
+        nc.vector.transpose(bi_all[:].rearrange("p b c -> p (b c)"), bi_wide[:].rearrange("p b c -> p (b c)"))
+        half_q = sb.tile([P, HALVES, I], F32, name="half_q", tag="x10")
+        bi_less_q = sb.tile([P, HALVES, I], F32, name="bi_less_q", tag="u0", align_bytes=64)
+        for h in range(HALVES):
+            rows_j = slice(h * P, (h + 1) * P)
+            q_bank = ps.tile([P, I], F32, name="q_bank", tag="bank%d" % h)
+            nc.tensor.matmul_mx(
+                out=q_bank[:],
+                lhsT=cx_w[:, rows_j].bitcast(E2M1),
+                lhsT_scale=cx_s[:, rows_j],
+                rhs=wc_w[:].bitcast(E4M3),
+                rhs_scale=wc_s[:],
+                start=True,
+                stop=True,
+            )
+            nc.vector.tensor_tensor(
+                bi_less_q[:, h, :].rearrange("p (c b) -> p c b", b=BI_RUN),
+                bi_all[:].rearrange("p b c -> p c b"),
+                q_bank[:].rearrange("p (c b) -> p c b", b=BI_RUN),
+                ALU.subtract,
+            )
+            nc.scalar.activation(half_q[:, h, :], q_bank[:], COPY, scale=0.5)
+        a_bank = [ps.tile([P, I], F32, name="a_bank", tag="bank%d" % h) for h in range(HALVES)]
+        for h in range(HALVES):
+            product(0, h)
+
+        for t in range(1, PACK):
+            late_plane(t)
+        for h in range(HALVES):
+            rows_j = slice(h * P, (h + 1) * P)
+            nc.vector.quantize_mx(
+                out=u_codes[:, 1, rows_j].bitcast(E5M2),
+                scales=u_scales[:, 1, rows_j],
+                in_=u1[h][:].rearrange("p j t -> p (j t)"),
+            )
+            product(1, h)
+
+        gap = sb.tile([P, HALVES, I], F32, name="gap")
+        kink = sb.tile([P, HALVES, I], F32, name="kink")
+        y = sb.tile([P, HALVES, I], F32, name="y")
+        for h in range(HALVES):
+            nc.vector.tensor_tensor(gap[:, h, :], a_bank[h][:], bi_less_q[:, h, :], ALU.add)
+        for h in range(HALVES):
+            nc.vector.scalar_tensor_tensor(kink[:, h, :], gap[:, h, :], -0.5, gap[:, h, :], ALU.mult, ALU.max)
+        for h in range(HALVES):
+            nc.vector.tensor_tensor(y[:, h, :], kink[:, h, :], half_q[:, h, :], ALU.add)
+            nc.sync.dma_start(out[h * P : (h + 1) * P, :], y[:, h, :])

@@ -22,7 +22,6 @@ PACK = 4
 PASSES = K // (P * PACK)
 HALVES = J // P
 PAD = 8
-LIST_COLS = P // 16
 QUAD = 32
 BI_RUN = I // QUAD
 
@@ -72,28 +71,29 @@ def tile_list_scores_steps_listed_tworank_kernel(
         for quad in range(4):
             load_scales(nc.gpsimd, cx_s, cx_scales, quad)
 
-        nc.sync.dma_start(tok[:], offs)
-        nc.sync.dma_start(key[:], offs2)
         nc.sync.dma_start(
             bi_runs[:], bi[0].rearrange("(c b) -> c b", b=BI_RUN).unsqueeze(0).to_broadcast([P // QUAD, QUAD, BI_RUN])
         )
-        for z in range(PASSES):
-            nc.sync.dma_start(ky_w[z][:].bitcast(I32), ky_words[z].bitcast(I32))
-        load_x(0)
+        nc.sync.dma_start(key[:], offs2)
+        nc.sync.dma_start(tok[:], offs)
+        nc.sync.dma_start(ky_w[0][:].bitcast(I32), ky_words[0].bitcast(I32))
         nc.sync.dma_start(fk_sb[:], fk.rearrange("(z p t) o -> p z (t o)", z=PASSES, t=PACK))
-        load_ky_scales(0)
-        load_ky_scales(1)
+        nc.sync.dma_start(ky_w[1][:].bitcast(I32), ky_words[1].bitcast(I32))
+        load_x(0)
         load_x(1)
-        load_ky_scales(2)
-        load_ky_scales(3)
-        load_scales(nc.sync, wc_s, wc_scales, 0)
+        for quad in range(4):
+            load_ky_scales(quad)
         load_x(2)
-        for quad in range(1, 4):
-            load_scales(nc.sync, wc_s, wc_scales, quad)
+        load_x(3)
         nc.sync.dma_start(cx_w[:].bitcast(I32), cx_words[0].bitcast(I32))
+        load_x(4)
+        for quad in range(3):
+            load_scales(nc.sync, wc_s, wc_scales, quad)
+        load_x(5)
+        load_scales(nc.sync, wc_s, wc_scales, 3)
         nc.sync.dma_start(wc_w[:].bitcast(I32), wc_words[0].rearrange("p n t -> p (n t)").bitcast(I32))
-        for n in range(3, 8):
-            load_x(n)
+        load_x(6)
+        load_x(7)
 
         u_codes = sb.tile([P, PASSES, J], U32, name="u_codes", align_bytes=64)
         u_scales = sb.tile([P, PASSES, J], U8, name="u_scales", align_bytes=64)
@@ -117,59 +117,75 @@ def tile_list_scores_steps_listed_tworank_kernel(
         for z in range(PASSES):
             nc.vector.tensor_copy(ky_sg[:, z, :], ky_s[:, z, :].indirect(key[:]))
 
-        raw = sb.tile([P, PACK, J], F32, name="raw")
-        u_flat = sb.tile([P, PACK, J], BF16, name="u_flat")
-        u0 = sb.tile([P, J, PACK], BF16, name="u0", align_bytes=64)
-        for t in range(PACK):
-            nc.scalar.activation(raw[:, t, :], x[0][t][:].indirect(tok[:]), COPY)
-            nc.scalar.activation(picked[:, t, PAD:], raw[:, t, :], COPY, scale=fk_sb[:, 0, t : t + 1])
-            nc.vector.scalar_tensor_tensor(
-                u_flat[:, t, :], picked[:, t, PAD - 1 : PAD - 1 + J], -0.6, picked[:, t, PAD:], ALU.mult, ALU.add
-            )
-            if t % 2 == 1:
-                nc.vector.tensor_copy(
-                    u0[:, :, t - 1 : t + 1].rearrange("p (c i) t -> p c t i", i=2),
-                    u_flat[:, t - 1 : t + 1, :].rearrange("p t (c i) -> p c t i", i=2),
-                )
-        nc.vector.quantize_mx(
-            out=u_codes[:, 0, :].bitcast(E5M2), scales=u_scales[:, 0, :], in_=u0[:].rearrange("p j t -> p (j t)")
+        bi_wide = sb.tile([P, BI_RUN, QUAD], F32, name="bi_wide", align_bytes=64)
+        bi_turned = sb.tile([P, BI_RUN, QUAD], F32, name="bi_turned", align_bytes=64)
+        bi_all = sb.tile([P, I], F32, name="bi_all")
+        nc.scalar.activation(bi_wide[:], bi_runs[:].unsqueeze(2).to_broadcast([P, BI_RUN, QUAD]), COPY)
+        nc.vector.transpose(bi_turned[:].rearrange("p b c -> p (b c)"), bi_wide[:].rearrange("p b c -> p (b c)"))
+        nc.scalar.activation(
+            bi_all[:].rearrange("p (c b) -> p c b", b=BI_RUN), bi_turned[:].rearrange("p b c -> p c b"), COPY
         )
 
-        step = sb.tile([P, PACK, J], F32, name="step")
+        u0 = sb.tile([P, J, PACK], BF16, name="u0", align_bytes=64)
         u1 = [sb.tile([P, P, PACK], BF16, name="u1_%d" % h, align_bytes=64) for h in range(HALVES)]
 
-        def late_plane(t):
-            row = picked[:, PACK + t, :]
-            for h in range(HALVES):
-                window = x[1][t][:].indirect(tok[:, h * LIST_COLS : (h + 1) * LIST_COLS])
-                dst = row[:, PAD + h * P : PAD + (h + 1) * P]
-                if t == PACK - 1 and h == 0:
+        last = PASSES * PACK - 1
+
+        def plane(n):
+            z, t = divmod(n, PACK)
+            factor = fk_sb[:, z, t : t + 1]
+            pieces = HALVES if n >= last - 1 else 1
+            width = J // pieces
+            row = picked[:, n, :]
+            step = sb.tile([P, J], F32, name="step%d" % n)
+            for h in range(pieces):
+                window = x[z][t][:].indirect(tok[:, h * width // 16 : (h + 1) * width // 16])
+                dst = row[:, PAD + h * width : PAD + (h + 1) * width]
+                if n == last and h == 0:
                     nc.vector.tensor_copy(dst, window)
                 else:
                     nc.scalar.activation(dst, window, COPY)
             for h in range(HALVES):
                 lo = PAD + h * P
                 nc.vector.scalar_tensor_tensor(
-                    step[:, t, h * P : (h + 1) * P], row[:, lo - 1 : lo - 1 + P], -0.6, row[:, lo : lo + P], ALU.mult, ALU.add
+                    step[:, h * P : (h + 1) * P], row[:, lo - 1 : lo - 1 + P], -0.6, row[:, lo : lo + P], ALU.mult, ALU.add
                 )
             for h in range(HALVES):
-                nc.vector.tensor_scalar(
-                    u1[h][:, :, t], step[:, t, h * P : (h + 1) * P], fk_sb[:, 1, t : t + 1], None, ALU.mult
-                )
+                cols = slice(h * P, (h + 1) * P)
+                dst = u0[:, cols, t] if z == 0 else u1[h][:, :, t]
+                if n == last and h == 1:
+                    nc.scalar.activation(dst, step[:, cols], COPY, scale=factor)
+                else:
+                    nc.vector.tensor_scalar(dst, step[:, cols], factor, None, ALU.mult)
 
-        late_plane(0)
+        raw = sb.tile([P, 2, J], F32, name="raw")
+        u_flat = sb.tile([P, 2, J], BF16, name="u_flat")
+        for t in range(2):
+            nc.scalar.activation(raw[:, t, :], x[0][t][:].indirect(tok[:]), COPY)
+            nc.scalar.activation(picked[:, t, PAD:], raw[:, t, :], COPY, scale=fk_sb[:, 0, t : t + 1])
+            nc.vector.scalar_tensor_tensor(
+                u_flat[:, t, :], picked[:, t, PAD - 1 : PAD - 1 + J], -0.6, picked[:, t, PAD:], ALU.mult, ALU.add
+            )
+        nc.vector.tensor_copy(
+            u0[:, :, 0:2].rearrange("p (c i) t -> p c t i", i=2), u_flat[:].rearrange("p t (c i) -> p c t i", i=2)
+        )
+        for n in range(2, PACK):
+            plane(n)
+        nc.vector.quantize_mx(
+            out=u_codes[:, 0, :].bitcast(E5M2), scales=u_scales[:, 0, :], in_=u0[:].rearrange("p j t -> p (j t)")
+        )
+        a_bank = [ps.tile([P, I], F32, name="a_bank%d" % h) for h in range(HALVES)]
+        for h in range(HALVES):
+            product(0, h)
+        plane(PACK)
+        plane(PACK + 1)
 
-        bi_wide = sb.tile([P, BI_RUN, QUAD], F32, name="bi_wide", align_bytes=64)
-        bi_all = sb.tile([P, BI_RUN, QUAD], F32, name="bi_all", align_bytes=64)
-        nc.vector.tensor_copy(bi_wide[:], bi_runs[:].unsqueeze(2).to_broadcast([P, BI_RUN, QUAD]))
-        nc.vector.transpose(bi_all[:].rearrange("p b c -> p (b c)"), bi_wide[:].rearrange("p b c -> p (b c)"))
-        half_q = sb.tile([P, HALVES, I], F32, name="half_q", tag="x10")
-        bi_less_q = sb.tile([P, HALVES, I], F32, name="bi_less_q", tag="u0", align_bytes=64)
+        q_bank = ps.tile([P, HALVES, I], F32, name="q_bank")
+        bi_less_q = sb.tile([P, HALVES, I], F32, name="bi_less_q")
         for h in range(HALVES):
             rows_j = slice(h * P, (h + 1) * P)
-            q_bank = ps.tile([P, I], F32, name="q_bank", tag="bank%d" % h)
             nc.tensor.matmul_mx(
-                out=q_bank[:],
+                out=q_bank[:, h, :],
                 lhsT=cx_w[:, rows_j].bitcast(E2M1),
                 lhsT_scale=cx_s[:, rows_j],
                 rhs=wc_w[:].bitcast(E4M3),
@@ -177,19 +193,10 @@ def tile_list_scores_steps_listed_tworank_kernel(
                 start=True,
                 stop=True,
             )
-            nc.vector.tensor_tensor(
-                bi_less_q[:, h, :].rearrange("p (c b) -> p c b", b=BI_RUN),
-                bi_all[:].rearrange("p b c -> p c b"),
-                q_bank[:].rearrange("p (c b) -> p c b", b=BI_RUN),
-                ALU.subtract,
-            )
-            nc.scalar.activation(half_q[:, h, :], q_bank[:], COPY, scale=0.5)
-        a_bank = [ps.tile([P, I], F32, name="a_bank", tag="bank%d" % h) for h in range(HALVES)]
-        for h in range(HALVES):
-            product(0, h)
+        nc.vector.tensor_tensor(bi_less_q[:], bi_all[:].unsqueeze(1).to_broadcast([P, HALVES, I]), q_bank[:], ALU.subtract)
 
-        for t in range(1, PACK):
-            late_plane(t)
+        for n in range(PACK + 2, PASSES * PACK):
+            plane(n)
         for h in range(HALVES):
             rows_j = slice(h * P, (h + 1) * P)
             nc.vector.quantize_mx(
@@ -207,5 +214,5 @@ def tile_list_scores_steps_listed_tworank_kernel(
         for h in range(HALVES):
             nc.vector.scalar_tensor_tensor(kink[:, h, :], gap[:, h, :], -0.5, gap[:, h, :], ALU.mult, ALU.max)
         for h in range(HALVES):
-            nc.vector.tensor_tensor(y[:, h, :], kink[:, h, :], half_q[:, h, :], ALU.add)
+            nc.vector.scalar_tensor_tensor(y[:, h, :], q_bank[:, h, :], 0.5, kink[:, h, :], ALU.mult, ALU.add)
             nc.sync.dma_start(out[h * P : (h + 1) * P, :], y[:, h, :])

@@ -1,6 +1,7 @@
 from contextlib import ExitStack
 
 import concourse.mybir as mybir
+from concourse.masks import make_identity
 
 K, T, J, I, V, L = 1024, 1024, 256, 256, 1024, 512
 FLOPS = 2 * K * J * I + 2 * L * J * I
@@ -20,10 +21,12 @@ COPY = mybir.ActivationFunctionType.Copy
 P = 128
 PACK = 4
 PASSES = K // (P * PACK)
+PLANES = PASSES * PACK
 HALVES = J // P
 PAD = 8
 QUAD = 32
-BI_RUN = I // QUAD
+LIVE = 4
+LIST_COLS = P // 16
 
 
 def tile_list_scores_steps_listed_tworank_kernel(
@@ -37,70 +40,108 @@ def tile_list_scores_steps_listed_tworank_kernel(
         tok = sb.tile([P, J // 16], U16, name="tok")
         key = sb.tile([P, I // 16], U16, name="key")
         fk_sb = sb.tile([P, PASSES, PACK], F32, name="fk_sb")
-        bi_runs = sb.tile([P, BI_RUN], F32, name="bi_runs")
-        x = [[sb.tile([P, T], F32, name="x%d%d" % (z, t)) for t in range(PACK)] for z in range(PASSES)]
+        bi_pairs = sb.tile([P, 2], F32, name="bi_pairs")
+        x = [sb.tile([P, T], F32, name="x%d" % n) for n in range(PLANES)]
         ky_w = [sb.tile([P, V], U16, name="ky_w%d" % z, align_bytes=64) for z in range(PASSES)]
-        ky_s = sb.tile([P, PASSES, V], U8, name="ky_s", align_bytes=64)
+        ky_s = sb.tile([P, PASSES, V], U8, name="ky_s", tag="step0")
         cx_w = sb.tile([P, J], U16, name="cx_w", align_bytes=64)
         wc_w = sb.tile([P, I], U32, name="wc_w", align_bytes=64)
-        cx_s = sb.tile([P, J], U8, name="cx_s", align_bytes=64)
-        wc_s = sb.tile([P, I], U8, name="wc_s", align_bytes=64)
-        picked = sb.tile([P, PASSES * PACK, PAD + J], F32, name="picked")
+        cx_s = sb.tile([P, 1, J], U8, name="cx_s", align_bytes=64)
+        wc_s = sb.tile([P, 1, I], U8, name="wc_s", align_bytes=64)
+        picked = sb.tile([P, PLANES, PAD + J], F32, name="picked")
+        ident = sb.tile([P, P], F32, name="ident")
 
-        nc.vector.memset(cx_s[:].bitcast(I32), 0)
-        nc.vector.memset(ky_s[:].rearrange("p z c -> p (z c)").bitcast(I32), 0)
-        nc.vector.memset(wc_s[:].bitcast(I32), 0)
+        for scale_tile in (ky_s, cx_s, wc_s):
+            nc.vector.memset(scale_tile[:].rearrange("p z c -> p (z c)").bitcast(I32), 0)
         nc.vector.memset(picked[:, :, PAD - 1 : PAD], 0.0)
+        make_identity(nc, ident[:])
 
-        rows = xf.rearrange("(z p t) w -> z t p w", z=PASSES, t=PACK)
+        planes_of_xf = xf.rearrange("(z p t) w -> z t p w", z=PASSES, t=PACK)
 
         def load_x(n):
-            nc.sync.dma_start(x[n // PACK][n % PACK][:], rows[n // PACK, n % PACK])
+            nc.sync.dma_start(x[n][:], planes_of_xf[n // PACK, n % PACK])
 
-        def load_scales(queue, plane, src, quad):
-            queue.dma_start(
-                plane[QUAD * quad : QUAD * quad + 4, :].bitcast(I32), src[0, 4 * quad : 4 * quad + 4, :].bitcast(I32)
-            )
-
-        def load_ky_scales(quad):
+        def load_scale_rows(tile, src, r):
             nc.sync.dma_start(
-                ky_s[QUAD * quad : QUAD * quad + 4, :, :].bitcast(I32),
-                ky_scales[:, 4 * quad : 4 * quad + 4, :].rearrange("z r c -> r z c").bitcast(I32),
+                tile[r:P:QUAD, :, :].bitcast(I32), src[:, r:16:LIVE, :].rearrange("z q c -> q z c").bitcast(I32)
             )
 
-        for quad in range(4):
-            load_scales(nc.gpsimd, cx_s, cx_scales, quad)
-
-        nc.sync.dma_start(
-            bi_runs[:], bi[0].rearrange("(c b) -> c b", b=BI_RUN).unsqueeze(0).to_broadcast([P // QUAD, QUAD, BI_RUN])
-        )
+        nc.sync.dma_start(bi_pairs[:], bi[0].rearrange("(p c) -> p c", c=2))
         nc.sync.dma_start(key[:], offs2)
         nc.sync.dma_start(tok[:], offs)
         nc.sync.dma_start(ky_w[0][:].bitcast(I32), ky_words[0].bitcast(I32))
         nc.sync.dma_start(fk_sb[:], fk.rearrange("(z p t) o -> p z (t o)", z=PASSES, t=PACK))
         nc.sync.dma_start(ky_w[1][:].bitcast(I32), ky_words[1].bitcast(I32))
         load_x(0)
-        load_x(1)
-        for quad in range(4):
-            load_ky_scales(quad)
-        load_x(2)
-        load_x(3)
-        nc.sync.dma_start(cx_w[:].bitcast(I32), cx_words[0].bitcast(I32))
+        for r in range(LIVE):
+            load_scale_rows(ky_s, ky_scales, r)
+        for n in range(1, PACK):
+            load_x(n)
+        for r in range(3):
+            load_scale_rows(cx_s, cx_scales, r)
         load_x(4)
-        for quad in range(3):
-            load_scales(nc.sync, wc_s, wc_scales, quad)
+        load_scale_rows(cx_s, cx_scales, 3)
+        load_scale_rows(wc_s, wc_scales, 0)
         load_x(5)
-        load_scales(nc.sync, wc_s, wc_scales, 3)
-        nc.sync.dma_start(wc_w[:].bitcast(I32), wc_words[0].rearrange("p n t -> p (n t)").bitcast(I32))
+        load_scale_rows(wc_s, wc_scales, 1)
         load_x(6)
+        load_scale_rows(wc_s, wc_scales, 2)
+        load_scale_rows(wc_s, wc_scales, 3)
         load_x(7)
+        nc.sync.dma_start(cx_w[:].bitcast(I32), cx_words[0].bitcast(I32))
+        nc.sync.dma_start(wc_w[:].bitcast(I32), wc_words[0].rearrange("p n t -> p (n t)").bitcast(I32))
 
-        u_codes = sb.tile([P, PASSES, J], U32, name="u_codes", align_bytes=64)
-        u_scales = sb.tile([P, PASSES, J], U8, name="u_scales", align_bytes=64)
+        bi_bank = ps.tile([P, 2, P], F32, name="bi_bank")
+        bi_all = sb.tile([P, I], F32, name="bi_all")
+        for c in range(2):
+            nc.tensor.transpose(bi_bank[:, c, :], bi_pairs[:, c : c + 1].to_broadcast([P, P]), ident[:])
+        nc.scalar.activation(
+            bi_all[:].rearrange("p (n c) -> p n c", c=2), bi_bank[:].rearrange("p c n -> p n c"), COPY
+        )
+
         ky_wg = [sb.tile([P, I], U16, name="ky_wg%d" % z, align_bytes=64) for z in range(PASSES)]
         ky_sg = sb.tile([P, PASSES, I], U8, name="ky_sg", align_bytes=64)
+        for z in range(PASSES):
+            nc.vector.tensor_copy(ky_wg[z][:], ky_w[z][:].indirect(key[:]))
+        for z in range(PASSES):
+            nc.vector.tensor_copy(ky_sg[:, z, :], ky_s[:, z, :].indirect(key[:]))
 
-        def product(z, h):
+        u0 = sb.tile([P, J, PACK], BF16, name="u0", align_bytes=64)
+        u1 = [sb.tile([P, P, PACK], BF16, name="u1_%d" % h, align_bytes=64) for h in range(HALVES)]
+        u_codes = sb.tile([P, PASSES, J], U32, name="u_codes", align_bytes=64)
+        u_scales = sb.tile([P, PASSES, J], U8, name="u_scales", align_bytes=64)
+        a_bank = [ps.tile([P, I], F32, name="a_bank%d" % h) for h in range(HALVES)]
+
+        def plane(n):
+            z, t = divmod(n, PACK)
+            is_last = n == PLANES - 1
+            factor = fk_sb[:, z, t : t + 1]
+            row = picked[:, n, :]
+            step = sb.tile([P, J], F32, name="step%d" % n)
+            if n < PLANES - 2:
+                nc.scalar.activation(row[:, PAD:], x[n][:].indirect(tok[:]), COPY)
+            else:
+                for h in range(HALVES):
+                    window = x[n][:].indirect(tok[:, h * LIST_COLS : (h + 1) * LIST_COLS])
+                    dst = row[:, PAD + h * P : PAD + (h + 1) * P]
+                    if is_last and h == 0:
+                        nc.vector.tensor_copy(dst, window)
+                    else:
+                        nc.scalar.activation(dst, window, COPY)
+            for h in range(HALVES):
+                lo = PAD + h * P
+                nc.vector.scalar_tensor_tensor(
+                    step[:, h * P : (h + 1) * P], row[:, lo - 1 : lo - 1 + P], -0.6, row[:, lo : lo + P], ALU.mult, ALU.add
+                )
+            for h in range(HALVES):
+                cols = slice(h * P, (h + 1) * P)
+                dst = u0[:, cols, t] if z == 0 else u1[h][:, :, t]
+                if is_last and h == 1:
+                    nc.scalar.activation(dst, step[:, cols], COPY, scale=factor)
+                else:
+                    nc.vector.tensor_scalar(dst, step[:, cols], factor, None, ALU.mult)
+
+        def first_score(z, h):
             rows_j = slice(h * P, (h + 1) * P)
             nc.tensor.matmul_mx(
                 out=a_bank[h][:],
@@ -112,91 +153,28 @@ def tile_list_scores_steps_listed_tworank_kernel(
                 stop=(z == PASSES - 1),
             )
 
-        for z in range(PASSES):
-            nc.vector.tensor_copy(ky_wg[z][:], ky_w[z][:].indirect(key[:]))
-        for z in range(PASSES):
-            nc.vector.tensor_copy(ky_sg[:, z, :], ky_s[:, z, :].indirect(key[:]))
-
-        bi_wide = sb.tile([P, BI_RUN, QUAD], F32, name="bi_wide", align_bytes=64)
-        bi_turned = sb.tile([P, BI_RUN, QUAD], F32, name="bi_turned", align_bytes=64)
-        bi_all = sb.tile([P, I], F32, name="bi_all")
-        nc.scalar.activation(bi_wide[:], bi_runs[:].unsqueeze(2).to_broadcast([P, BI_RUN, QUAD]), COPY)
-        nc.vector.transpose(bi_turned[:].rearrange("p b c -> p (b c)"), bi_wide[:].rearrange("p b c -> p (b c)"))
-        nc.scalar.activation(
-            bi_all[:].rearrange("p (c b) -> p c b", b=BI_RUN), bi_turned[:].rearrange("p b c -> p c b"), COPY
-        )
-
-        u0 = sb.tile([P, J, PACK], BF16, name="u0", align_bytes=64)
-        u1 = [sb.tile([P, P, PACK], BF16, name="u1_%d" % h, align_bytes=64) for h in range(HALVES)]
-
-        last = PASSES * PACK - 1
-
-        def plane(n):
-            z, t = divmod(n, PACK)
-            factor = fk_sb[:, z, t : t + 1]
-            pieces = HALVES if n >= last - 1 else 1
-            width = J // pieces
-            row = picked[:, n, :]
-            step = sb.tile([P, J], F32, name="step%d" % n)
-            for h in range(pieces):
-                window = x[z][t][:].indirect(tok[:, h * width // 16 : (h + 1) * width // 16])
-                dst = row[:, PAD + h * width : PAD + (h + 1) * width]
-                if n == last and h == 0:
-                    nc.vector.tensor_copy(dst, window)
-                else:
-                    nc.scalar.activation(dst, window, COPY)
-            for h in range(HALVES):
-                lo = PAD + h * P
-                nc.vector.scalar_tensor_tensor(
-                    step[:, h * P : (h + 1) * P], row[:, lo - 1 : lo - 1 + P], -0.6, row[:, lo : lo + P], ALU.mult, ALU.add
-                )
-            for h in range(HALVES):
-                cols = slice(h * P, (h + 1) * P)
-                dst = u0[:, cols, t] if z == 0 else u1[h][:, :, t]
-                if n == last and h == 1:
-                    nc.scalar.activation(dst, step[:, cols], COPY, scale=factor)
-                else:
-                    nc.vector.tensor_scalar(dst, step[:, cols], factor, None, ALU.mult)
-
-        raw = sb.tile([P, 2, J], F32, name="raw")
-        u_flat = sb.tile([P, 2, J], BF16, name="u_flat")
-        for t in range(2):
-            nc.scalar.activation(raw[:, t, :], x[0][t][:].indirect(tok[:]), COPY)
-            nc.scalar.activation(picked[:, t, PAD:], raw[:, t, :], COPY, scale=fk_sb[:, 0, t : t + 1])
-            nc.vector.scalar_tensor_tensor(
-                u_flat[:, t, :], picked[:, t, PAD - 1 : PAD - 1 + J], -0.6, picked[:, t, PAD:], ALU.mult, ALU.add
-            )
-        nc.vector.tensor_copy(
-            u0[:, :, 0:2].rearrange("p (c i) t -> p c t i", i=2), u_flat[:].rearrange("p t (c i) -> p c t i", i=2)
-        )
-        for n in range(2, PACK):
+        for n in range(PACK):
             plane(n)
         nc.vector.quantize_mx(
             out=u_codes[:, 0, :].bitcast(E5M2), scales=u_scales[:, 0, :], in_=u0[:].rearrange("p j t -> p (j t)")
         )
-        a_bank = [ps.tile([P, I], F32, name="a_bank%d" % h) for h in range(HALVES)]
         for h in range(HALVES):
-            product(0, h)
-        plane(PACK)
-        plane(PACK + 1)
+            first_score(0, h)
+        for n in range(PACK, PLANES):
+            plane(n)
 
         q_bank = ps.tile([P, HALVES, I], F32, name="q_bank")
-        bi_less_q = sb.tile([P, HALVES, I], F32, name="bi_less_q")
         for h in range(HALVES):
             rows_j = slice(h * P, (h + 1) * P)
             nc.tensor.matmul_mx(
                 out=q_bank[:, h, :],
                 lhsT=cx_w[:, rows_j].bitcast(E2M1),
-                lhsT_scale=cx_s[:, rows_j],
+                lhsT_scale=cx_s[:, 0, rows_j],
                 rhs=wc_w[:].bitcast(E4M3),
-                rhs_scale=wc_s[:],
+                rhs_scale=wc_s[:, 0, :],
                 start=True,
                 stop=True,
             )
-        nc.vector.tensor_tensor(bi_less_q[:], bi_all[:].unsqueeze(1).to_broadcast([P, HALVES, I]), q_bank[:], ALU.subtract)
-
-        for n in range(PACK + 2, PASSES * PACK):
-            plane(n)
         for h in range(HALVES):
             rows_j = slice(h * P, (h + 1) * P)
             nc.vector.quantize_mx(
@@ -204,7 +182,9 @@ def tile_list_scores_steps_listed_tworank_kernel(
                 scales=u_scales[:, 1, rows_j],
                 in_=u1[h][:].rearrange("p j t -> p (j t)"),
             )
-            product(1, h)
+            first_score(1, h)
+        bi_less_q = sb.tile([P, HALVES, I], F32, name="bi_less_q", tag="u1_1", align_bytes=64)
+        nc.vector.tensor_tensor(bi_less_q[:], bi_all[:].unsqueeze(1).to_broadcast([P, HALVES, I]), q_bank[:], ALU.subtract)
 
         gap = sb.tile([P, HALVES, I], F32, name="gap")
         kink = sb.tile([P, HALVES, I], F32, name="kink")

@@ -51,9 +51,11 @@ def tile_list_scores_steps_listed_tworank_kernel(
         picked = sb.tile([P, PLANES, PAD + J], F32, name="picked")
         ident = sb.tile([P, P], F32, name="ident")
 
+        zeros = sb.tile([P, PLANES], F32, name="zeros")
+        nc.vector.memset(zeros[:], 0.0)
+        nc.scalar.activation(picked[:, :, PAD - 1], zeros[:], COPY)
         for scale_tile in (ky_s, cx_s, wc_s):
             nc.vector.memset(scale_tile[:].rearrange("p z c -> p (z c)").bitcast(I32), 0)
-        nc.vector.memset(picked[:, :, PAD - 1 : PAD], 0.0)
         make_identity(nc, ident[:])
 
         planes_of_xf = xf.rearrange("(z p t) w -> z t p w", z=PASSES, t=PACK)
@@ -66,10 +68,9 @@ def tile_list_scores_steps_listed_tworank_kernel(
                 tile[r:P:QUAD, :, :].bitcast(I32), src[:, r:16:LIVE, :].rearrange("z q c -> q z c").bitcast(I32)
             )
 
-        nc.sync.dma_start(bi_pairs[:], bi[0].rearrange("(p c) -> p c", c=2))
         nc.sync.dma_start(key[:], offs2)
-        nc.sync.dma_start(tok[:], offs)
         nc.sync.dma_start(ky_w[0][:].bitcast(I32), ky_words[0].bitcast(I32))
+        nc.sync.dma_start(tok[:], offs)
         nc.sync.dma_start(fk_sb[:], fk.rearrange("(z p t) o -> p z (t o)", z=PASSES, t=PACK))
         nc.sync.dma_start(ky_w[1][:].bitcast(I32), ky_words[1].bitcast(I32))
         load_x(0)
@@ -77,17 +78,12 @@ def tile_list_scores_steps_listed_tworank_kernel(
             load_scale_rows(ky_s, ky_scales, r)
         for n in range(1, PACK):
             load_x(n)
-        for r in range(3):
-            load_scale_rows(cx_s, cx_scales, r)
-        load_x(4)
-        load_scale_rows(cx_s, cx_scales, 3)
-        load_scale_rows(wc_s, wc_scales, 0)
-        load_x(5)
-        load_scale_rows(wc_s, wc_scales, 1)
-        load_x(6)
-        load_scale_rows(wc_s, wc_scales, 2)
-        load_scale_rows(wc_s, wc_scales, 3)
-        load_x(7)
+        nc.sync.dma_start(bi_pairs[:], bi[0].rearrange("(p c) -> p c", c=2))
+        for n in range(PACK, PLANES):
+            scale_tile, src = (cx_s, cx_scales) if n < PACK + 2 else (wc_s, wc_scales)
+            for r in (2 * (n % 2), 2 * (n % 2) + 1):
+                load_scale_rows(scale_tile, src, r)
+            load_x(n)
         nc.sync.dma_start(cx_w[:].bitcast(I32), cx_words[0].bitcast(I32))
         nc.sync.dma_start(wc_w[:].bitcast(I32), wc_words[0].rearrange("p n t -> p (n t)").bitcast(I32))
 
@@ -136,10 +132,7 @@ def tile_list_scores_steps_listed_tworank_kernel(
             for h in range(HALVES):
                 cols = slice(h * P, (h + 1) * P)
                 dst = u0[:, cols, t] if z == 0 else u1[h][:, :, t]
-                if is_last and h == 1:
-                    nc.scalar.activation(dst, step[:, cols], COPY, scale=factor)
-                else:
-                    nc.vector.tensor_scalar(dst, step[:, cols], factor, None, ALU.mult)
+                nc.vector.tensor_scalar(dst, step[:, cols], factor, None, ALU.mult)
 
         def first_score(z, h):
             rows_j = slice(h * P, (h + 1) * P)

from contextlib import ExitStack

import concourse.mybir as mybir
from concourse.masks import make_identity

K, T, J, I, V, L = 1024, 1024, 256, 256, 1024, 512
FLOPS = 2 * K * J * I + 2 * L * J * I

F32 = mybir.dt.float32
BF16 = mybir.dt.bfloat16
I32 = mybir.dt.int32
U32 = mybir.dt.uint32
U16 = mybir.dt.uint16
U8 = mybir.dt.uint8
E5M2 = mybir.dt.float8_e5m2_x4
E4M3 = mybir.dt.float8_e4m3fn_x4
E2M1 = mybir.dt.float4_e2m1fn_x4
ALU = mybir.AluOpType
COPY = mybir.ActivationFunctionType.Copy

P = 128
PACK = 4
PASSES = K // (P * PACK)
PLANES = PASSES * PACK
HALVES = J // P
PAD = 8
QUAD = 32
LIVE = 4
LIST_COLS = P // 16


def tile_list_scores_steps_listed_tworank_kernel(
    tc, xf, fk, ky_words, ky_scales, bi, cx_words, cx_scales, wc_words, wc_scales, offs, offs2, out
):
    nc = tc.nc
    with ExitStack() as ctx:
        sb = ctx.enter_context(tc.tile_pool(name="sb", bufs=1))
        ps = ctx.enter_context(tc.psum_pool(name="ps", bufs=1))

        tok = sb.tile([P, J // 16], U16, name="tok")
        key = sb.tile([P, I // 16], U16, name="key")
        fk_sb = sb.tile([P, PASSES, PACK], F32, name="fk_sb")
        bi_pairs = sb.tile([P, 2], F32, name="bi_pairs")
        x = [sb.tile([P, T], F32, name="x%d" % n) for n in range(PLANES)]
        ky_w = [sb.tile([P, V], U16, name="ky_w%d" % z, align_bytes=64) for z in range(PASSES)]
        ky_s = sb.tile([P, PASSES, V], U8, name="ky_s", tag="step0")
        cx_w = sb.tile([P, J], U16, name="cx_w", align_bytes=64)
        wc_w = sb.tile([P, I], U32, name="wc_w", align_bytes=64)
        cx_s = sb.tile([P, 1, J], U8, name="cx_s", align_bytes=64)
        wc_s = sb.tile([P, 1, I], U8, name="wc_s", align_bytes=64)
        picked = sb.tile([P, PLANES, PAD + J], F32, name="picked")
        ident = sb.tile([P, P], F32, name="ident")

        zeros = sb.tile([P, PLANES], F32, name="zeros")
        nc.vector.memset(zeros[:], 0.0)
        nc.scalar.activation(picked[:, :, PAD - 1], zeros[:], COPY)
        for scale_tile in (ky_s, cx_s, wc_s):
            nc.vector.memset(scale_tile[:].rearrange("p z c -> p (z c)").bitcast(I32), 0)
        make_identity(nc, ident[:])

        planes_of_xf = xf.rearrange("(z p t) w -> z t p w", z=PASSES, t=PACK)

        def load_x(n):
            nc.sync.dma_start(x[n][:], planes_of_xf[n // PACK, n % PACK])

        def load_scale_rows(tile, src, r):
            nc.sync.dma_start(
                tile[r:P:QUAD, :, :].bitcast(I32), src[:, r:16:LIVE, :].rearrange("z q c -> q z c").bitcast(I32)
            )

        nc.sync.dma_start(key[:], offs2)
        nc.sync.dma_start(ky_w[0][:].bitcast(I32), ky_words[0].bitcast(I32))
        nc.sync.dma_start(tok[:], offs)
        nc.sync.dma_start(fk_sb[:], fk.rearrange("(z p t) o -> p z (t o)", z=PASSES, t=PACK))
        nc.sync.dma_start(ky_w[1][:].bitcast(I32), ky_words[1].bitcast(I32))
        load_x(0)
        for r in range(LIVE):
            load_scale_rows(ky_s, ky_scales, r)
        for n in range(1, PACK):
            load_x(n)
        nc.sync.dma_start(bi_pairs[:], bi[0].rearrange("(p c) -> p c", c=2))
        for n in range(PACK, PLANES):
            scale_tile, src = (cx_s, cx_scales) if n < PACK + 2 else (wc_s, wc_scales)
            for r in (2 * (n % 2), 2 * (n % 2) + 1):
                load_scale_rows(scale_tile, src, r)
            load_x(n)
        nc.sync.dma_start(cx_w[:].bitcast(I32), cx_words[0].bitcast(I32))
        nc.sync.dma_start(wc_w[:].bitcast(I32), wc_words[0].rearrange("p n t -> p (n t)").bitcast(I32))

        bi_bank = ps.tile([P, 2, P], F32, name="bi_bank")
        bi_all = sb.tile([P, I], F32, name="bi_all")
        for c in range(2):
            nc.tensor.transpose(bi_bank[:, c, :], bi_pairs[:, c : c + 1].to_broadcast([P, P]), ident[:])
        nc.scalar.activation(
            bi_all[:].rearrange("p (n c) -> p n c", c=2), bi_bank[:].rearrange("p c n -> p n c"), COPY
        )

        ky_wg = [sb.tile([P, I], U16, name="ky_wg%d" % z, align_bytes=64) for z in range(PASSES)]
        ky_sg = sb.tile([P, PASSES, I], U8, name="ky_sg", align_bytes=64)
        for z in range(PASSES):
            nc.vector.tensor_copy(ky_wg[z][:], ky_w[z][:].indirect(key[:]))
        for z in range(PASSES):
            nc.vector.tensor_copy(ky_sg[:, z, :], ky_s[:, z, :].indirect(key[:]))

        u0 = sb.tile([P, J, PACK], BF16, name="u0", align_bytes=64)
        u1 = [sb.tile([P, P, PACK], BF16, name="u1_%d" % h, align_bytes=64) for h in range(HALVES)]
        u_codes = sb.tile([P, PASSES, J], U32, name="u_codes", align_bytes=64)
        u_scales = sb.tile([P, PASSES, J], U8, name="u_scales", align_bytes=64)
        a_bank = [ps.tile([P, I], F32, name="a_bank%d" % h) for h in range(HALVES)]

        def plane(n):
            z, t = divmod(n, PACK)
            is_last = n == PLANES - 1
            factor = fk_sb[:, z, t : t + 1]
            row = picked[:, n, :]
            step = sb.tile([P, J], F32, name="step%d" % n)
            if n < PLANES - 2:
                nc.scalar.activation(row[:, PAD:], x[n][:].indirect(tok[:]), COPY)
            else:
                for h in range(HALVES):
                    window = x[n][:].indirect(tok[:, h * LIST_COLS : (h + 1) * LIST_COLS])
                    dst = row[:, PAD + h * P : PAD + (h + 1) * P]
                    if is_last and h == 0:
                        nc.vector.tensor_copy(dst, window)
                    else:
                        nc.scalar.activation(dst, window, COPY)
            for h in range(HALVES):
                lo = PAD + h * P
                nc.vector.scalar_tensor_tensor(
                    step[:, h * P : (h + 1) * P], row[:, lo - 1 : lo - 1 + P], -0.6, row[:, lo : lo + P], ALU.mult, ALU.add
                )
            for h in range(HALVES):
                cols = slice(h * P, (h + 1) * P)
                dst = u0[:, cols, t] if z == 0 else u1[h][:, :, t]
                nc.vector.tensor_scalar(dst, step[:, cols], factor, None, ALU.mult)

        def first_score(z, h):
            rows_j = slice(h * P, (h + 1) * P)
            nc.tensor.matmul_mx(
                out=a_bank[h][:],
                lhsT=u_codes[:, z, rows_j].bitcast(E5M2),
                lhsT_scale=u_scales[:, z, rows_j],
                rhs=ky_wg[z][:].bitcast(E2M1),
                rhs_scale=ky_sg[:, z, :],
                start=(z == 0),
                stop=(z == PASSES - 1),
            )

        for n in range(PACK):
            plane(n)
        nc.vector.quantize_mx(
            out=u_codes[:, 0, :].bitcast(E5M2), scales=u_scales[:, 0, :], in_=u0[:].rearrange("p j t -> p (j t)")
        )
        for h in range(HALVES):
            first_score(0, h)
        for n in range(PACK, PLANES):
            plane(n)

        q_bank = ps.tile([P, HALVES, I], F32, name="q_bank")
        for h in range(HALVES):
            rows_j = slice(h * P, (h + 1) * P)
            nc.tensor.matmul_mx(
                out=q_bank[:, h, :],
                lhsT=cx_w[:, rows_j].bitcast(E2M1),
                lhsT_scale=cx_s[:, 0, rows_j],
                rhs=wc_w[:].bitcast(E4M3),
                rhs_scale=wc_s[:, 0, :],
                start=True,
                stop=True,
            )
        for h in range(HALVES):
            rows_j = slice(h * P, (h + 1) * P)
            nc.vector.quantize_mx(
                out=u_codes[:, 1, rows_j].bitcast(E5M2),
                scales=u_scales[:, 1, rows_j],
                in_=u1[h][:].rearrange("p j t -> p (j t)"),
            )
            first_score(1, h)
        bi_less_q = sb.tile([P, HALVES, I], F32, name="bi_less_q", tag="u1_1", align_bytes=64)
        nc.vector.tensor_tensor(bi_less_q[:], bi_all[:].unsqueeze(1).to_broadcast([P, HALVES, I]), q_bank[:], ALU.subtract)

        gap = sb.tile([P, HALVES, I], F32, name="gap")
        kink = sb.tile([P, HALVES, I], F32, name="kink")
        y = sb.tile([P, HALVES, I], F32, name="y")
        for h in range(HALVES):
            nc.vector.tensor_tensor(gap[:, h, :], a_bank[h][:], bi_less_q[:, h, :], ALU.add)
        for h in range(HALVES):
            nc.vector.scalar_tensor_tensor(kink[:, h, :], gap[:, h, :], -0.5, gap[:, h, :], ALU.mult, ALU.max)
        for h in range(HALVES):
            nc.vector.scalar_tensor_tensor(y[:, h, :], q_bank[:, h, :], 0.5, kink[:, h, :], ALU.mult, ALU.add)
            nc.sync.dma_start(out[h * P : (h + 1) * P, :], y[:, h, :])
